import numpy as np
import ml_dtypes


def mxq(x, axis, fmt="e4m3"):
    dtype, down = {"e4m3": (ml_dtypes.float8_e4m3fn, 7), "e5m2": (ml_dtypes.float8_e5m2, 14)}[fmt]
    v = np.moveaxis(np.asarray(x, np.float32).astype(ml_dtypes.bfloat16).astype(np.float64), axis, -1)
    blocks = v.reshape(v.shape[:-1] + (-1, 32))
    amax = np.abs(blocks).max(-1, keepdims=True)
    byte = np.maximum(np.where(amax > 0, np.frexp(amax)[1] - 1 + 127, 0) - down, 1)
    scale = np.exp2(byte - 127.0)
    codes = (blocks / scale).astype(np.float32).astype(dtype).astype(np.float64)
    return np.moveaxis((codes * scale).reshape(v.shape), -1, axis)


WIDE = False


def mx_kscale(k):
    if not WIDE:
        return np.ones(k)
    levels = np.array([10, -10, 5, -5, 0])
    if k % 512:
        return np.exp2(np.random.permutation(np.resize(levels, k // 32))).repeat(32)
    a = np.empty((k // 512, 16))
    for p in range(k // 512):
        a[p, :8] = np.random.permutation(np.resize(levels, 8))
        for g in range(8):
            far = levels[np.abs(levels - a[p, g]) >= 10]
            a[p, g + 8] = far[np.random.randint(len(far))]
    return np.exp2(a.ravel()).repeat(32)


def f64(x):
    return np.asarray(x).astype(np.float64)


def striped(idx):
    return np.tile(np.asarray(idx).reshape(-1, 16).T, (8, 1)).astype(np.uint16)


def unstriped(offs):
    return offs[:16].T.reshape(-1).astype(np.int64)


def striped8(idx):
    return np.asarray(idx).reshape(8, -1, 16).transpose(0, 2, 1).reshape(128, -1).astype(np.uint16)


def unstriped8(offs):
    return offs.reshape(8, 16, -1).transpose(0, 2, 1).reshape(8, -1).astype(np.int64)


def pick8(x, idx, run):
    r = np.arange(len(x))
    return x[r[:, None], idx[r % (8 * run) // run]]


E2M1 = np.array([0.0, 0.5, 1.0, 1.5, 2.0, 3.0, 4.0, 6.0, -0.0, -0.5, -1.0, -1.5, -2.0, -3.0, -4.0, -6.0])


def pack_weight(w, fmt):
    k, n = w.shape
    w = f64(np.asarray(w, np.float32).astype(ml_dtypes.bfloat16)).reshape(k // 32, 32, n)
    amax = np.abs(w).max(1)
    if fmt == "e4m3":
        byte = np.frexp(amax)[1] - 1 + 127 - 7
    else:
        mant, ex = np.frexp(amax / 6.0)
        byte = np.where(mant > 0.5, ex, ex - 1) + 127
    byte = np.clip(np.where(amax > 0, byte, 1), 1, 254)
    scaled = (w * np.exp2(127.0 - byte)[:, None, :]).reshape(k, n).astype(np.float32)
    by_word = np.ascontiguousarray(scaled.reshape(k // 512, 128, 4, n).transpose(0, 1, 3, 2))
    if fmt == "e4m3":
        words = by_word.astype(ml_dtypes.float8_e4m3fn).view(np.uint8)
    else:
        c = by_word.astype(ml_dtypes.float4_e2m1fn).view(np.uint8) & 0xF
        words = (c[..., 0::2] | (c[..., 1::2] << 4)).reshape(k // 512, 128, 2 * n)
    return np.ascontiguousarray(words), np.ascontiguousarray(byte.astype(np.uint8).reshape(k // 512, 16, n))


def unpack_weight(words, scales, fmt):
    g, _, n = scales.shape
    words = np.ascontiguousarray(words).reshape(g, 128, n, -1)
    if fmt == "e4m3":
        vals = words.view(ml_dtypes.float8_e4m3fn).astype(np.float64)
    else:
        nib = np.empty((g, 128, n, 4), np.uint8)
        nib[..., 0::2] = words & 0xF
        nib[..., 1::2] = words >> 4
        vals = E2M1[nib]
    vals = vals * np.repeat(np.exp2(scales.astype(np.float64) - 127.0), 8, axis=1)[..., None]
    return vals.transpose(0, 1, 3, 2).reshape(g * 512, n)


K, J, R, T, U, F, O, N, E = 512, 512, 512, 2048, 1024, 1024, 256, 256, 128


def setup_inputs():
    n = np.random.standard_normal
    idx = np.stack([np.random.permutation(T)[:J] for _ in range(8)])
    idx2 = np.stack([np.random.permutation(U)[:J] for _ in range(8)])
    idx3 = np.stack([np.random.permutation(U)[:J] for _ in range(8)])
    idx4 = np.random.permutation(F)[:R]
    idx5 = np.stack([np.random.permutation(J)[:O] for _ in range(8)])
    idx6 = np.stack([np.random.permutation(O)[:E] for _ in range(8)])
    idx7 = np.stack([np.random.permutation(O)[:E] for _ in range(8)])
    fk = mx_kscale(K)
    fr = mx_kscale(R)
    tr = np.ones(F)
    tr[idx4] = fr
    wtp = pack_weight(n((K, F)) * 1 / np.sqrt(K) / fk[:, None] * tr, "e4m3")
    wbp = pack_weight(n((R, N)) * 1 / np.sqrt(R) / fr[:, None], "e2m1")
    wop = pack_weight(n((R, N)) * 1 / np.sqrt(R) / fr[:, None], "e4m3")
    return {
        "ta": (np.random.randint(-7, 8, (K, T)).astype(np.float64)).astype(np.float32),
        "ga": ((np.random.randint(8, 25, (K, 1)) / 64.0) * fk[:, None]).astype(np.float32),
        "gb": (np.random.uniform(0.5, 1.6, (K, 1))).astype(np.float32),
        "wt_words": wtp[0],
        "wt_scales": wtp[1],
        "sa": (np.random.uniform(0.5, 1.6, (R, 1))).astype(np.float32),
        "wb_words": wbp[0],
        "wb_scales": wbp[1],
        "wo_words": wop[0],
        "wo_scales": wop[1],
        "so": (np.random.uniform(0.5, 1.6, (N, 1))).astype(np.float32),
        "sp": (np.random.uniform(0.5, 1.6, (N, 1))).astype(np.float32),
        "offs": striped8(idx),
        "offs2": striped8(idx2),
        "offs3": striped8(idx3),
        "offs4": striped(idx4),
        "offs5": striped8(idx5),
        "offs6": striped8(idx6),
        "offs7": striped8(idx7),
    }


def reference(ta, ga, gb, wt_words, wt_scales, sa, wb_words, wb_scales, wo_words, wo_scales, so, sp, offs, offs2, offs3, offs4, offs5, offs6, offs7):
    idx = unstriped8(offs)
    idx2 = unstriped8(offs2)
    idx3 = unstriped8(offs3)
    idx4 = unstriped(offs4)
    idx5 = unstriped8(offs5)
    idx6 = unstriped8(offs6)
    idx7 = unstriped8(offs7)
    wtu = unpack_weight(wt_words, wt_scales, "e4m3")
    wbu = unpack_weight(wb_words, wb_scales, "e2m1")
    wou = unpack_weight(wo_words, wo_scales, "e4m3")
    xcd = pick8(f64(ta), idx, 64) * f64(ga)
    xcp = np.zeros((K, U))
    xcp[np.arange(K)[:, None], idx2[np.arange(K) % 512 // 64]] = xcd
    xc = pick8(xcp, idx3, 64) * f64(gb)
    wtidx4g = wtu[:, idx4]
    xcq = mxq(xc, 0, "e4m3")
    a = wtidx4g.T @ xcq
    g1 = np.maximum(a, 0.0)
    hid = pick8(g1, idx5, 64) * f64(sa)
    hidq = mxq(hid, 0, "e4m3")
    p = wbu.T @ hidq
    q = wou.T @ hidq
    y = pick8(p, idx6, 16) * f64(so) - pick8(q, idx7, 16) * f64(sp)
    return y

@@ -1,0 +1,208 @@
+from contextlib import ExitStack
+
+import concourse.mybir as mybir
+
+K, J, R, T, U, F, O, N, E = 512, 512, 512, 2048, 1024, 1024, 256, 256, 128
+FLOPS = 2 * K * R * J + 2 * 2 * R * N * O
+
+F32 = mybir.dt.float32
+BF16 = mybir.dt.bfloat16
+I32 = mybir.dt.int32
+U32 = mybir.dt.uint32
+U16 = mybir.dt.uint16
+U8 = mybir.dt.uint8
+FP8X4 = mybir.dt.float8_e4m3fn_x4
+FP4X4 = mybir.dt.float4_e2m1fn_x4
+ACT = mybir.ActivationFunctionType
+ALU = mybir.AluOpType
+
+P = 128
+PACK = 4
+QUADS = 4
+HALVES = 2
+RUN = 4
+ALIGN = 64
+SPLIT_TILES = 2
+
+
+def load_list(nc, pool, offs, name):
+    tile = pool.tile(list(offs.shape), U16, name=name)
+    nc.sync.dma_start(tile[:], offs)
+    return tile
+
+
+def load_dealt(queue, pool, vec, name):
+    tile = pool.tile([P, PACK], F32, name=name)
+    queue.dma_start(tile[:], vec.rearrange("(p t) o -> p (t o)", t=PACK))
+    return tile
+
+
+def load_by_block(nc, pool, vec, name):
+    tile = pool.tile([P, N // P], F32, name=name)
+    with nc.allow_non_contiguous_dma(reason="one value a partition and block of rows"):
+        nc.sync.dma_start(tile[:], vec.rearrange("(u p) o -> p (u o)", p=P))
+    return tile
+
+
+def load_scale_rows(nc, plane, scales):
+    for q in range(QUADS):
+        nc.sync.dma_start(plane[32 * q : 32 * q + 4, :].bitcast(I32), scales[0, 4 * q : 4 * q + 4, :].bitcast(I32))
+
+
+def interleave(copy, woven, planes):
+    copy(
+        woven.rearrange("p (c i t) -> p c t i", i=RUN, t=PACK),
+        planes.rearrange("p t (c i) -> p c t i", i=RUN),
+    )
+
+
+def tile_picked_codepage_store_one_kept_outcomes_outmeet_kernel(
+    tc, ta, ga, gb, wt_words, wt_scales, sa, wb_words, wb_scales, wo_words, wo_scales, so, sp,
+    offs, offs2, offs3, offs4, offs5, offs6, offs7, out,
+):
+    nc = tc.nc
+    jh, oh = J // HALVES, O // HALVES
+
+    with ExitStack() as ctx:
+        lists = ctx.enter_context(tc.tile_pool(name="lists", bufs=1))
+        keep = ctx.enter_context(tc.tile_pool(name="keep", bufs=1))
+        psum = ctx.enter_context(tc.psum_pool(name="psum", bufs=1))
+
+        ta_rows = ta.rearrange("(p t) c -> t p c", t=PACK)
+        table = [keep.tile([P, T], F32, name="table%d" % t, tag="table%d" % t, align_bytes=ALIGN) for t in range(PACK)]
+        wts_stage = keep.tile([4, QUADS, F // 4], I32, name="wts_stage")
+        nc.scalar.dma_start(wts_stage[:], wt_scales[0].bitcast(I32).rearrange("(q i) c -> i q c", i=4))
+        ga_t = load_dealt(nc.scalar, keep, ga, "ga_t")
+        l4 = load_list(nc, lists, offs4, "l4")
+        l1 = load_list(nc, lists, offs, "l1")
+        nc.sync.dma_start(table[0][:], ta_rows[0])
+        l2 = load_list(nc, lists, offs2, "l2")
+        for t in range(1, PACK):
+            nc.sync.dma_start(table[t][:], ta_rows[t])
+        l3 = load_list(nc, lists, offs3, "l3")
+        gb_t = load_dealt(nc.sync, keep, gb, "gb_t")
+
+        wts_window = keep.tile([P, F], U8, name="wts_window")
+        wb_plane = keep.tile([P, N], U8, name="wb_plane", align_bytes=ALIGN)
+        wo_plane = keep.tile([P, N], U8, name="wo_plane", align_bytes=ALIGN)
+        page = [keep.tile([P, U], F32, name="page%d" % t) for t in range(PACK)]
+        nc.vector.memset(wts_window[:].bitcast(I32), 0)
+        nc.vector.memset(wb_plane[:].bitcast(I32), 0)
+        nc.vector.memset(wo_plane[:].bitcast(I32), 0)
+        for t in range(PACK):
+            nc.vector.memset(page[t][:], 0.0)
+
+        wtw_window = keep.tile([P, F], I32, name="wtw_window")
+        nc.sync.dma_start(wtw_window[:], wt_words[0].rearrange("p c b -> p (c b)").bitcast(I32))
+        l5 = load_list(nc, lists, offs5, "l5")
+        sa_t = load_dealt(nc.sync, keep, sa, "sa_t")
+        wb_codes = keep.tile([P, 2 * N], U8, name="wb_codes", align_bytes=ALIGN)
+        nc.sync.dma_start(wb_codes[:].bitcast(I32), wb_words[0].bitcast(I32))
+        wo_codes = keep.tile([P, N], I32, name="wo_codes", align_bytes=ALIGN)
+        nc.sync.dma_start(wo_codes[:], wo_words[0].rearrange("p c b -> p (c b)").bitcast(I32))
+        load_scale_rows(nc, wb_plane, wb_scales)
+        load_scale_rows(nc, wo_plane, wo_scales)
+        l6 = load_list(nc, lists, offs6, "l6")
+        l7 = load_list(nc, lists, offs7, "l7")
+        so_t = load_by_block(nc, keep, so, "so_t")
+        sp_t = load_by_block(nc, keep, sp, "sp_t")
+
+        for q in range(QUADS):
+            nc.vector.tensor_copy(wts_window[32 * q : 32 * q + 4, :].bitcast(I32), wts_stage[:, q, :])
+        wt_plane = keep.tile([P, R], U8, name="wt_plane", align_bytes=ALIGN)
+        nc.vector.tensor_copy(
+            wt_plane[:].rearrange("p (t m) -> p m t", t=PACK), wts_window[:].indirect(l4[:])
+        )
+
+        xcd = [keep.tile([P, J], F32, name="xcd%d" % t, tag="xcd%d" % t, align_bytes=ALIGN) for t in range(PACK)]
+        for t in range(PACK):
+            nc.scalar.activation(xcd[t][:], table[t][:].indirect(l1[:]), ACT.Copy, scale=ga_t[:, t : t + 1])
+            nc.vector.tensor_copy(page[t][:].indirect(l2[:]), xcd[t][:])
+
+        xc = keep.tile([P, HALVES, PACK, jh], BF16, name="xc", tag="table%d" % (PACK - 1), align_bytes=ALIGN)
+        cols3 = jh // 16
+        for t in range(PACK):
+            for h in range(HALVES):
+                nc.scalar.activation(
+                    xc[:, h, t, :], page[t][:].indirect(l3[:, h * cols3 : (h + 1) * cols3]), ACT.Copy,
+                    scale=gb_t[:, t : t + 1],
+                )
+
+        wt_codes = keep.tile([P, R], U32, name="wt_codes", tag="xcd%d" % (PACK - 1), align_bytes=ALIGN)
+        nc.vector.tensor_copy(
+            wt_codes[:].rearrange("p (t m) -> p m t", t=PACK), wtw_window[:].bitcast(U32).indirect(l4[:])
+        )
+
+        xc_woven = [keep.tile([P, PACK * jh], BF16, name="xc_woven%d" % h, align_bytes=ALIGN) for h in range(HALVES)]
+        xc_codes = keep.tile([P, J], U32, name="xc_codes", align_bytes=ALIGN)
+        xc_plane = keep.tile([P, J], U8, name="xc_plane", align_bytes=ALIGN)
+        interleave(nc.vector.tensor_copy, xc_woven[0][:], xc[:, 0])
+        interleave(nc.scalar.copy, xc_woven[1][:], xc[:, 1])
+        for h in range(HALVES):
+            slots = slice(h * jh, (h + 1) * jh)
+            nc.vector.quantize_mx(out=xc_codes[:, slots].bitcast(FP8X4), scales=xc_plane[:, slots], in_=xc_woven[h][:])
+
+        g1 = [keep.tile([P, J], F32, name="g1_%d" % t) for t in range(PACK)]
+        hid = keep.tile([P, HALVES, PACK, oh], BF16, name="hid", align_bytes=ALIGN)
+
+        def hidden(t, slots, bank):
+            acc = psum.tile([P, slots.stop - slots.start], F32, name="acc", tag="bank%d" % bank)
+            nc.tensor.matmul_mx(
+                out=acc[:],
+                lhsT=wt_codes[:, t * P : (t + 1) * P].bitcast(FP8X4),
+                lhsT_scale=wt_plane[:, t * P : (t + 1) * P],
+                rhs=xc_codes[:, slots].bitcast(FP8X4),
+                rhs_scale=xc_plane[:, slots],
+                start=True,
+                stop=True,
+            )
+            return acc
+
+        first, second, whole = slice(0, jh), slice(jh, J), slice(0, J)
+        for t in range(SPLIT_TILES):
+            nc.scalar.activation(g1[t][:, first], hidden(t, first, t)[:], ACT.Relu)
+        for t in range(SPLIT_TILES):
+            nc.vector.tensor_scalar_max(g1[t][:, second], hidden(t, second, PACK + t)[:], 0.0)
+        for t in range(SPLIT_TILES, PACK):
+            nc.vector.tensor_scalar_max(g1[t][:], hidden(t, whole, t)[:], 0.0)
+        cols5 = oh // 16
+        for t in range(PACK):
+            for h in range(HALVES):
+                nc.scalar.activation(
+                    hid[:, h, t, :], g1[t][:].indirect(l5[:, h * cols5 : (h + 1) * cols5]), ACT.Copy,
+                    scale=sa_t[:, t : t + 1],
+                )
+
+        hid_woven = [keep.tile([P, PACK * oh], BF16, name="hid_woven%d" % h, align_bytes=ALIGN) for h in range(HALVES)]
+        hid_codes = keep.tile([P, O], U32, name="hid_codes", align_bytes=ALIGN)
+        hid_plane = keep.tile([P, O], U8, name="hid_plane", align_bytes=ALIGN)
+        for h in range(HALVES):
+            interleave(nc.vector.tensor_copy, hid_woven[h][:], hid[:, h])
+        for h in range(HALVES):
+            nc.vector.quantize_mx(
+                out=hid_codes[:, h * oh : (h + 1) * oh].bitcast(FP8X4),
+                scales=hid_plane[:, h * oh : (h + 1) * oh],
+                in_=hid_woven[h][:],
+            )
+
+        for u in range(N // P):
+            rows = slice(u * P, (u + 1) * P)
+            sides = (
+                (wb_codes[:, 2 * u * P : 2 * (u + 1) * P].bitcast(FP4X4), wb_plane, l6, so_t),
+                (wo_codes[:, rows].bitcast(FP8X4), wo_plane, l7, sp_t),
+            )
+            picked = []
+            for s, (codes, plane, places, weight) in enumerate(sides):
+                acc = psum.tile([P, O], F32, name="acc", tag="bank%d" % ((6 + 2 * u + s) % 8))
+                nc.tensor.matmul_mx(
+                    out=acc[:], lhsT=codes, lhsT_scale=plane[:, rows],
+                    rhs=hid_codes[:].bitcast(FP8X4), rhs_scale=hid_plane[:], start=True, stop=True,
+                )
+                outcome = keep.tile([P, O], F32, name="outcome%d%d" % (u, s))
+                nc.vector.tensor_copy(outcome[:], acc[:])
+                got = keep.tile([P, E], F32, name="got%d%d" % (u, s))
+                nc.scalar.activation(got[:], outcome[:].indirect(places[:]), ACT.Copy, scale=weight[:, u : u + 1])
+                picked.append(got)
+            y = keep.tile([P, E], F32, name="y%d" % u)
+            nc.vector.tensor_tensor(y[:], picked[0][:], picked[1][:], ALU.subtract)
+            nc.sync.dma_start(out[rows, :], y[:])

@@ -73,6 +73,9 @@ def tile_picked_codepage_store_one_kept_outcomes_outmeet_kernel(
         wts_stage = keep.tile([4, QUADS, F // 4], I32, name="wts_stage")
         nc.scalar.dma_start(wts_stage[:], wt_scales[0].bitcast(I32).rearrange("(q i) c -> i q c", i=4))
         ga_t = load_dealt(nc.scalar, keep, ga, "ga_t")
+        warm = keep.tile([P, 8], F32, name="warm")
+        nc.vector.memset(warm[:, 0:1], 0.0)
+        nc.scalar.activation(warm[:, 1:2], warm[:, 0:1], ACT.Copy)
         l4 = load_list(nc, lists, offs4, "l4")
         l1 = load_list(nc, lists, offs, "l1")
         nc.sync.dma_start(table[0][:], ta_rows[0])

@@ -22,7 +22,8 @@ QUADS = 4
 HALVES = 2
 RUN = 4
 ALIGN = 64
-SPLIT_TILES = 2
+PAGES = 3
+QUARTERS = 4
 
 
 def load_list(nc, pool, offs, name):
@@ -49,10 +50,10 @@ def load_scale_rows(nc, plane, scales):
         nc.sync.dma_start(plane[32 * q : 32 * q + 4, :].bitcast(I32), scales[0, 4 * q : 4 * q + 4, :].bitcast(I32))
 
 
-def interleave(copy, woven, planes):
+def interleave(copy, woven, planes, rows=slice(0, PACK)):
     copy(
-        woven.rearrange("p (c i t) -> p c t i", i=RUN, t=PACK),
-        planes.rearrange("p t (c i) -> p c t i", i=RUN),
+        woven.rearrange("p (c i t) -> p c t i", i=RUN, t=PACK)[:, :, rows, :],
+        planes[:, rows, :].rearrange("p t (c i) -> p c t i", i=RUN),
     )
 
 
@@ -70,15 +71,16 @@ def tile_picked_codepage_store_one_kept_outcomes_outmeet_kernel(
 
         ta_rows = ta.rearrange("(p t) c -> t p c", t=PACK)
         table = [keep.tile([P, T], F32, name="table%d" % t, tag="table%d" % t, align_bytes=ALIGN) for t in range(PACK)]
-        wts_stage = keep.tile([4, QUADS, F // 4], I32, name="wts_stage")
-        nc.scalar.dma_start(wts_stage[:], wt_scales[0].bitcast(I32).rearrange("(q i) c -> i q c", i=4))
-        ga_t = load_dealt(nc.scalar, keep, ga, "ga_t")
+        nc.scalar.dma_start(table[0][:, : T // 2], ta_rows[0][:, : T // 2])
         warm = keep.tile([P, 8], F32, name="warm")
         nc.vector.memset(warm[:, 0:1], 0.0)
         nc.scalar.activation(warm[:, 1:2], warm[:, 0:1], ACT.Copy)
+        wts_stage = keep.tile([4, QUADS, F // 4], I32, name="wts_stage")
+        nc.sync.dma_start(wts_stage[:], wt_scales[0].bitcast(I32).rearrange("(q i) c -> i q c", i=4))
         l4 = load_list(nc, lists, offs4, "l4")
         l1 = load_list(nc, lists, offs, "l1")
-        nc.sync.dma_start(table[0][:], ta_rows[0])
+        ga_t = load_dealt(nc.sync, keep, ga, "ga_t")
+        nc.sync.dma_start(table[0][:, T // 2 :], ta_rows[0][:, T // 2 :])
         l2 = load_list(nc, lists, offs2, "l2")
         for t in range(1, PACK):
             nc.sync.dma_start(table[t][:], ta_rows[t])
@@ -88,12 +90,12 @@ def tile_picked_codepage_store_one_kept_outcomes_outmeet_kernel(
         wts_window = keep.tile([P, F], U8, name="wts_window")
         wb_plane = keep.tile([P, N], U8, name="wb_plane", align_bytes=ALIGN)
         wo_plane = keep.tile([P, N], U8, name="wo_plane", align_bytes=ALIGN)
-        page = [keep.tile([P, U], F32, name="page%d" % t) for t in range(PACK)]
+        page = [keep.tile([P, U], F32, name="page%d" % t) for t in range(PAGES)]
         nc.vector.memset(wts_window[:].bitcast(I32), 0)
         nc.vector.memset(wb_plane[:].bitcast(I32), 0)
         nc.vector.memset(wo_plane[:].bitcast(I32), 0)
-        for t in range(PACK):
-            nc.vector.memset(page[t][:], 0.0)
+        for t in range(PAGES):
+            nc.vector.memset(page[t][:].bitcast(I32), 0)
 
         wtw_window = keep.tile([P, F], I32, name="wtw_window")
         nc.sync.dma_start(wtw_window[:], wt_words[0].rearrange("p c b -> p (c b)").bitcast(I32))
@@ -120,30 +122,38 @@ def tile_picked_codepage_store_one_kept_outcomes_outmeet_kernel(
         xcd = [keep.tile([P, J], F32, name="xcd%d" % t, tag="xcd%d" % t, align_bytes=ALIGN) for t in range(PACK)]
         for t in range(PACK):
             nc.scalar.activation(xcd[t][:], table[t][:].indirect(l1[:]), ACT.Copy, scale=ga_t[:, t : t + 1])
-            nc.vector.tensor_copy(page[t][:].indirect(l2[:]), xcd[t][:])
 
         xc = keep.tile([P, HALVES, PACK, jh], BF16, name="xc", tag="table%d" % (PACK - 1), align_bytes=ALIGN)
         cols3 = jh // 16
+        jq = J // QUARTERS
+        xc_woven = [keep.tile([P, PACK * jq], BF16, name="xc_woven%d" % c, align_bytes=ALIGN) for c in range(QUARTERS)]
+
+        def weave_pair(copies, rows):
+            for c in range(QUARTERS):
+                h, first = divmod(c * jq, jh)
+                interleave(copies[h], xc_woven[c][:], xc[:, h, :, first : first + jq], rows)
+
         for t in range(PACK):
+            nc.vector.tensor_copy(page[t % PAGES][:].indirect(l2[:]), xcd[t][:])
             for h in range(HALVES):
                 nc.scalar.activation(
-                    xc[:, h, t, :], page[t][:].indirect(l3[:, h * cols3 : (h + 1) * cols3]), ACT.Copy,
+                    xc[:, h, t, :], page[t % PAGES][:].indirect(l3[:, h * cols3 : (h + 1) * cols3]), ACT.Copy,
                     scale=gb_t[:, t : t + 1],
                 )
+            if t == 1:
+                weave_pair((nc.scalar.copy, nc.scalar.copy), slice(0, 2))
 
         wt_codes = keep.tile([P, R], U32, name="wt_codes", tag="xcd%d" % (PACK - 1), align_bytes=ALIGN)
         nc.vector.tensor_copy(
             wt_codes[:].rearrange("p (t m) -> p m t", t=PACK), wtw_window[:].bitcast(U32).indirect(l4[:])
         )
 
-        xc_woven = [keep.tile([P, PACK * jh], BF16, name="xc_woven%d" % h, align_bytes=ALIGN) for h in range(HALVES)]
         xc_codes = keep.tile([P, J], U32, name="xc_codes", align_bytes=ALIGN)
         xc_plane = keep.tile([P, J], U8, name="xc_plane", align_bytes=ALIGN)
-        interleave(nc.vector.tensor_copy, xc_woven[0][:], xc[:, 0])
-        interleave(nc.scalar.copy, xc_woven[1][:], xc[:, 1])
-        for h in range(HALVES):
-            slots = slice(h * jh, (h + 1) * jh)
-            nc.vector.quantize_mx(out=xc_codes[:, slots].bitcast(FP8X4), scales=xc_plane[:, slots], in_=xc_woven[h][:])
+        weave_pair((nc.vector.tensor_copy, nc.scalar.copy), slice(2, PACK))
+        for c in range(QUARTERS):
+            slots = slice(c * jq, (c + 1) * jq)
+            nc.vector.quantize_mx(out=xc_codes[:, slots].bitcast(FP8X4), scales=xc_plane[:, slots], in_=xc_woven[c][:])
 
         g1 = [keep.tile([P, J], F32, name="g1_%d" % t) for t in range(PACK)]
         hid = keep.tile([P, HALVES, PACK, oh], BF16, name="hid", align_bytes=ALIGN)
@@ -161,13 +171,16 @@ def tile_picked_codepage_store_one_kept_outcomes_outmeet_kernel(
             )
             return acc
 
-        first, second, whole = slice(0, jh), slice(jh, J), slice(0, J)
-        for t in range(SPLIT_TILES):
-            nc.scalar.activation(g1[t][:, first], hidden(t, first, t)[:], ACT.Relu)
-        for t in range(SPLIT_TILES):
-            nc.vector.tensor_scalar_max(g1[t][:, second], hidden(t, second, PACK + t)[:], 0.0)
-        for t in range(SPLIT_TILES, PACK):
-            nc.vector.tensor_scalar_max(g1[t][:], hidden(t, whole, t)[:], 0.0)
+        cuts = ((0, jh, jh + jq, J), (0, jh, J), (0, J), (0, J))
+        bank = 0
+        for t in range(PACK):
+            for lo, hi in zip(cuts[t], cuts[t][1:]):
+                acc = hidden(t, slice(lo, hi), bank)
+                if bank == 0:
+                    nc.scalar.activation(g1[t][:, lo:hi], acc[:], ACT.Relu)
+                else:
+                    nc.vector.tensor_scalar_max(g1[t][:, lo:hi], acc[:], 0.0)
+                bank = bank + 1
         cols5 = oh // 16
         for t in range(PACK):
             for h in range(HALVES):
@@ -196,13 +209,16 @@ def tile_picked_codepage_store_one_kept_outcomes_outmeet_kernel(
             )
             picked = []
             for s, (codes, plane, places, weight) in enumerate(sides):
-                acc = psum.tile([P, O], F32, name="acc", tag="bank%d" % ((6 + 2 * u + s) % 8))
-                nc.tensor.matmul_mx(
-                    out=acc[:], lhsT=codes, lhsT_scale=plane[:, rows],
-                    rhs=hid_codes[:].bitcast(FP8X4), rhs_scale=hid_plane[:], start=True, stop=True,
-                )
                 outcome = keep.tile([P, O], F32, name="outcome%d%d" % (u, s))
-                nc.vector.tensor_copy(outcome[:], acc[:])
+                parts = (0, oh, O) if u == 0 and s == 0 else (0, O)
+                for lo, hi in zip(parts, parts[1:]):
+                    acc = psum.tile([P, hi - lo], F32, name="acc", tag="bank%d" % (bank % 8))
+                    nc.tensor.matmul_mx(
+                        out=acc[:], lhsT=codes, lhsT_scale=plane[:, rows],
+                        rhs=hid_codes[:, lo:hi].bitcast(FP8X4), rhs_scale=hid_plane[:, lo:hi], start=True, stop=True,
+                    )
+                    (nc.scalar.copy if hi < O else nc.vector.tensor_copy)(outcome[:, lo:hi], acc[:])
+                    bank = bank + 1
                 got = keep.tile([P, E], F32, name="got%d%d" % (u, s))
                 nc.scalar.activation(got[:], outcome[:].indirect(places[:]), ACT.Copy, scale=weight[:, u : u + 1])
                 picked.append(got)

from contextlib import ExitStack

import concourse.mybir as mybir

K, J, R, T, U, F, O, N, E = 512, 512, 512, 2048, 1024, 1024, 256, 256, 128
FLOPS = 2 * K * R * J + 2 * 2 * R * N * O

F32 = mybir.dt.float32
BF16 = mybir.dt.bfloat16
I32 = mybir.dt.int32
U32 = mybir.dt.uint32
U16 = mybir.dt.uint16
U8 = mybir.dt.uint8
FP8X4 = mybir.dt.float8_e4m3fn_x4
FP4X4 = mybir.dt.float4_e2m1fn_x4
ACT = mybir.ActivationFunctionType
ALU = mybir.AluOpType

P = 128
PACK = 4
QUADS = 4
HALVES = 2
RUN = 4
ALIGN = 64
PAGES = 3
QUARTERS = 4


def load_list(nc, pool, offs, name):
    tile = pool.tile(list(offs.shape), U16, name=name)
    nc.sync.dma_start(tile[:], offs)
    return tile


def load_dealt(queue, pool, vec, name):
    tile = pool.tile([P, PACK], F32, name=name)
    queue.dma_start(tile[:], vec.rearrange("(p t) o -> p (t o)", t=PACK))
    return tile


def load_by_block(nc, pool, vec, name):
    tile = pool.tile([P, N // P], F32, name=name)
    with nc.allow_non_contiguous_dma(reason="one value a partition and block of rows"):
        nc.sync.dma_start(tile[:], vec.rearrange("(u p) o -> p (u o)", p=P))
    return tile


def load_scale_rows(nc, plane, scales):
    for q in range(QUADS):
        nc.sync.dma_start(plane[32 * q : 32 * q + 4, :].bitcast(I32), scales[0, 4 * q : 4 * q + 4, :].bitcast(I32))


def interleave(copy, woven, planes, rows=slice(0, PACK)):
    copy(
        woven.rearrange("p (c i t) -> p c t i", i=RUN, t=PACK)[:, :, rows, :],
        planes[:, rows, :].rearrange("p t (c i) -> p c t i", i=RUN),
    )


def tile_picked_codepage_store_one_kept_outcomes_outmeet_kernel(
    tc, ta, ga, gb, wt_words, wt_scales, sa, wb_words, wb_scales, wo_words, wo_scales, so, sp,
    offs, offs2, offs3, offs4, offs5, offs6, offs7, out,
):
    nc = tc.nc
    jh, oh = J // HALVES, O // HALVES

    with ExitStack() as ctx:
        lists = ctx.enter_context(tc.tile_pool(name="lists", bufs=1))
        keep = ctx.enter_context(tc.tile_pool(name="keep", bufs=1))
        psum = ctx.enter_context(tc.psum_pool(name="psum", bufs=1))

        ta_rows = ta.rearrange("(p t) c -> t p c", t=PACK)
        table = [keep.tile([P, T], F32, name="table%d" % t, tag="table%d" % t, align_bytes=ALIGN) for t in range(PACK)]
        nc.scalar.dma_start(table[0][:, : T // 2], ta_rows[0][:, : T // 2])
        warm = keep.tile([P, 8], F32, name="warm")
        nc.vector.memset(warm[:, 0:1], 0.0)
        nc.scalar.activation(warm[:, 1:2], warm[:, 0:1], ACT.Copy)
        wts_stage = keep.tile([4, QUADS, F // 4], I32, name="wts_stage")
        nc.sync.dma_start(wts_stage[:], wt_scales[0].bitcast(I32).rearrange("(q i) c -> i q c", i=4))
        l4 = load_list(nc, lists, offs4, "l4")
        l1 = load_list(nc, lists, offs, "l1")
        ga_t = load_dealt(nc.sync, keep, ga, "ga_t")
        nc.sync.dma_start(table[0][:, T // 2 :], ta_rows[0][:, T // 2 :])
        l2 = load_list(nc, lists, offs2, "l2")
        for t in range(1, PACK):
            nc.sync.dma_start(table[t][:], ta_rows[t])
        l3 = load_list(nc, lists, offs3, "l3")
        gb_t = load_dealt(nc.sync, keep, gb, "gb_t")

        wts_window = keep.tile([P, F], U8, name="wts_window")
        wb_plane = keep.tile([P, N], U8, name="wb_plane", align_bytes=ALIGN)
        wo_plane = keep.tile([P, N], U8, name="wo_plane", align_bytes=ALIGN)
        page = [keep.tile([P, U], F32, name="page%d" % t) for t in range(PAGES)]
        nc.vector.memset(wts_window[:].bitcast(I32), 0)
        nc.vector.memset(wb_plane[:].bitcast(I32), 0)
        nc.vector.memset(wo_plane[:].bitcast(I32), 0)
        for t in range(PAGES):
            nc.vector.memset(page[t][:].bitcast(I32), 0)

        wtw_window = keep.tile([P, F], I32, name="wtw_window")
        nc.sync.dma_start(wtw_window[:], wt_words[0].rearrange("p c b -> p (c b)").bitcast(I32))
        l5 = load_list(nc, lists, offs5, "l5")
        sa_t = load_dealt(nc.sync, keep, sa, "sa_t")
        wb_codes = keep.tile([P, 2 * N], U8, name="wb_codes", align_bytes=ALIGN)
        nc.sync.dma_start(wb_codes[:].bitcast(I32), wb_words[0].bitcast(I32))
        wo_codes = keep.tile([P, N], I32, name="wo_codes", align_bytes=ALIGN)
        nc.sync.dma_start(wo_codes[:], wo_words[0].rearrange("p c b -> p (c b)").bitcast(I32))
        load_scale_rows(nc, wb_plane, wb_scales)
        load_scale_rows(nc, wo_plane, wo_scales)
        l6 = load_list(nc, lists, offs6, "l6")
        l7 = load_list(nc, lists, offs7, "l7")
        so_t = load_by_block(nc, keep, so, "so_t")
        sp_t = load_by_block(nc, keep, sp, "sp_t")

        for q in range(QUADS):
            nc.vector.tensor_copy(wts_window[32 * q : 32 * q + 4, :].bitcast(I32), wts_stage[:, q, :])
        wt_plane = keep.tile([P, R], U8, name="wt_plane", align_bytes=ALIGN)
        nc.vector.tensor_copy(
            wt_plane[:].rearrange("p (t m) -> p m t", t=PACK), wts_window[:].indirect(l4[:])
        )

        xcd = [keep.tile([P, J], F32, name="xcd%d" % t, tag="xcd%d" % t, align_bytes=ALIGN) for t in range(PACK)]
        for t in range(PACK):
            nc.scalar.activation(xcd[t][:], table[t][:].indirect(l1[:]), ACT.Copy, scale=ga_t[:, t : t + 1])

        xc = keep.tile([P, HALVES, PACK, jh], BF16, name="xc", tag="table%d" % (PACK - 1), align_bytes=ALIGN)
        cols3 = jh // 16
        jq = J // QUARTERS
        xc_woven = [keep.tile([P, PACK * jq], BF16, name="xc_woven%d" % c, align_bytes=ALIGN) for c in range(QUARTERS)]

        def weave_pair(copies, rows):
            for c in range(QUARTERS):
                h, first = divmod(c * jq, jh)
                interleave(copies[h], xc_woven[c][:], xc[:, h, :, first : first + jq], rows)

        for t in range(PACK):
            nc.vector.tensor_copy(page[t % PAGES][:].indirect(l2[:]), xcd[t][:])
            for h in range(HALVES):
                nc.scalar.activation(
                    xc[:, h, t, :], page[t % PAGES][:].indirect(l3[:, h * cols3 : (h + 1) * cols3]), ACT.Copy,
                    scale=gb_t[:, t : t + 1],
                )
            if t == 1:
                weave_pair((nc.scalar.copy, nc.scalar.copy), slice(0, 2))

        wt_codes = keep.tile([P, R], U32, name="wt_codes", tag="xcd%d" % (PACK - 1), align_bytes=ALIGN)
        nc.vector.tensor_copy(
            wt_codes[:].rearrange("p (t m) -> p m t", t=PACK), wtw_window[:].bitcast(U32).indirect(l4[:])
        )

        xc_codes = keep.tile([P, J], U32, name="xc_codes", align_bytes=ALIGN)
        xc_plane = keep.tile([P, J], U8, name="xc_plane", align_bytes=ALIGN)
        weave_pair((nc.vector.tensor_copy, nc.scalar.copy), slice(2, PACK))
        for c in range(QUARTERS):
            slots = slice(c * jq, (c + 1) * jq)
            nc.vector.quantize_mx(out=xc_codes[:, slots].bitcast(FP8X4), scales=xc_plane[:, slots], in_=xc_woven[c][:])

        g1 = [keep.tile([P, J], F32, name="g1_%d" % t) for t in range(PACK)]
        hid = keep.tile([P, HALVES, PACK, oh], BF16, name="hid", align_bytes=ALIGN)

        def hidden(t, slots, bank):
            acc = psum.tile([P, slots.stop - slots.start], F32, name="acc", tag="bank%d" % bank)
            nc.tensor.matmul_mx(
                out=acc[:],
                lhsT=wt_codes[:, t * P : (t + 1) * P].bitcast(FP8X4),
                lhsT_scale=wt_plane[:, t * P : (t + 1) * P],
                rhs=xc_codes[:, slots].bitcast(FP8X4),
                rhs_scale=xc_plane[:, slots],
                start=True,
                stop=True,
            )
            return acc

        cuts = ((0, jh, jh + jq, J), (0, jh, J), (0, J), (0, J))
        bank = 0
        for t in range(PACK):
            for lo, hi in zip(cuts[t], cuts[t][1:]):
                acc = hidden(t, slice(lo, hi), bank)
                if bank == 0:
                    nc.scalar.activation(g1[t][:, lo:hi], acc[:], ACT.Relu)
                else:
                    nc.vector.tensor_scalar_max(g1[t][:, lo:hi], acc[:], 0.0)
                bank = bank + 1
        cols5 = oh // 16
        for t in range(PACK):
            for h in range(HALVES):
                nc.scalar.activation(
                    hid[:, h, t, :], g1[t][:].indirect(l5[:, h * cols5 : (h + 1) * cols5]), ACT.Copy,
                    scale=sa_t[:, t : t + 1],
                )

        hid_woven = [keep.tile([P, PACK * oh], BF16, name="hid_woven%d" % h, align_bytes=ALIGN) for h in range(HALVES)]
        hid_codes = keep.tile([P, O], U32, name="hid_codes", align_bytes=ALIGN)
        hid_plane = keep.tile([P, O], U8, name="hid_plane", align_bytes=ALIGN)
        for h in range(HALVES):
            interleave(nc.vector.tensor_copy, hid_woven[h][:], hid[:, h])
        for h in range(HALVES):
            nc.vector.quantize_mx(
                out=hid_codes[:, h * oh : (h + 1) * oh].bitcast(FP8X4),
                scales=hid_plane[:, h * oh : (h + 1) * oh],
                in_=hid_woven[h][:],
            )

        for u in range(N // P):
            rows = slice(u * P, (u + 1) * P)
            sides = (
                (wb_codes[:, 2 * u * P : 2 * (u + 1) * P].bitcast(FP4X4), wb_plane, l6, so_t),
                (wo_codes[:, rows].bitcast(FP8X4), wo_plane, l7, sp_t),
            )
            picked = []
            for s, (codes, plane, places, weight) in enumerate(sides):
                outcome = keep.tile([P, O], F32, name="outcome%d%d" % (u, s))
                parts = (0, oh, O) if u == 0 and s == 0 else (0, O)
                for lo, hi in zip(parts, parts[1:]):
                    acc = psum.tile([P, hi - lo], F32, name="acc", tag="bank%d" % (bank % 8))
                    nc.tensor.matmul_mx(
                        out=acc[:], lhsT=codes, lhsT_scale=plane[:, rows],
                        rhs=hid_codes[:, lo:hi].bitcast(FP8X4), rhs_scale=hid_plane[:, lo:hi], start=True, stop=True,
                    )
                    (nc.scalar.copy if hi < O else nc.vector.tensor_copy)(outcome[:, lo:hi], acc[:])
                    bank = bank + 1
                got = keep.tile([P, E], F32, name="got%d%d" % (u, s))
                nc.scalar.activation(got[:], outcome[:].indirect(places[:]), ACT.Copy, scale=weight[:, u : u + 1])
                picked.append(got)
            y = keep.tile([P, E], F32, name="y%d" % u)
            nc.vector.tensor_tensor(y[:], picked[0][:], picked[1][:], ALU.subtract)
            nc.sync.dma_start(out[rows, :], y[:])
